import numpy as np, ml_dtypes
CORES = [21,109,149,237,277,365,405,493,150,406]
N = 10
import mx_ref
NC, GR, GC, T = 128, 5, 2, 10
TA, TB = T // GC, T // GR
BF = ml_dtypes.bfloat16
def setup_inputs(rng):
    def f(*shape):
        return mx_ref.flush((rng.standard_normal(shape, dtype=np.float32) * np.exp2(rng.integers(-2, 3, shape[:-1] + (1,)))).astype(BF))
    return {"a": f(N, 128, TA * 512), "b": f(N, 128, TB * 4 * NC)}
def setup_inputs_blocks(rng):
    d = setup_inputs(rng)
    for k in ("a", "b"): d[k] = mx_ref.spread(d[k], rng, 2)
    return d
def setup_inputs_wide(rng):
    d = setup_inputs(rng)
    for k in ("a", "b"): d[k] = mx_ref.flush((d[k].astype(np.float32) * np.exp2(rng.integers(-8, 9, (N, 1, 1))).astype(np.float32)).astype(BF))
    return d
def setup_inputs_zeros(rng):
    d = setup_inputs(rng); v = d["b"].reshape(N, 128, -1, 4).copy()
    v[np.broadcast_to((rng.random((N, 1, v.shape[2], 1)) < 0.33), v.shape)] = 0
    d["b"] = v.reshape(d["b"].shape)
    return d
def reference(a, b):
    A = lambda i, s: mx_ref.quantize(a[i * GC + s // TA][:, 512 * (s % TA):512 * (s % TA) + 512])
    B = lambda s, j: mx_ref.quantize(b[(s // TB) * GC + j][:, 4 * NC * (s % TB):4 * NC * (s % TB) + 4 * NC])
    y = np.zeros((N, 128, NC), np.float32)
    for r in range(N):
        for s in range(T):
            p = mx_ref.matmul(A(r // GC, s), B(s, r % GC))
            y[r] = p if s == 0 else y[r] + p
    return {"y": y}

@@ -1,0 +1,245 @@
+from concourse.bass import DstId, RemoteDMATransfer
+from concourse.mybir import dt
+
+WORLD = 512
+GR, GC, NS = 5, 2, 10
+TA, TB, W = NS // GC, NS // GR, 128
+A1 = 2
+
+SCRATCH = {
+    "abf": ("sbuf", [128, TA * 4 * W], "bfloat16"),
+    "bbf": ("sbuf", [128, TB * 4 * W], "bfloat16"),
+    "qa": ("sbuf", [128, NS * W], "float8_e4m3fn_x4"),
+    "sa": ("sbuf", [128, NS * W], "uint8"),
+    "qb": ("sbuf", [128, NS * W], "float8_e4m3fn_x4"),
+    "sb": ("sbuf", [128, NS * W], "uint8"),
+    "ps": ("psum", [128, 512], "float32"),
+    "yo": ("sbuf", [128, W], "float32"),
+}
+SEMAPHORES = ["la1", "lb", "la2", "za1", "zb", "za2", "a1", "a2", "b0", "b1", "b2", "b3", "b4", "ls", "mm", "cp", "st"]
+
+_CACHE = {}
+
+
+def _bits(m):
+    return [i for i in range(m.bit_length()) if (m >> i) & 1]
+
+
+def make_plan(cores, topo):
+    n = len(cores)
+    used = set(cores)
+    place = lambda c: (topo.host(c), topo.chip(c))
+    rack = lambda c: topo.rack(topo.host(c))
+
+    def take(pred):
+        for c in range(WORLD):
+            if c not in used and pred(c):
+                used.add(c)
+                return c
+        return None
+
+    ops, total, offm = {}, {}, {}
+
+    def off_mask(src):
+        if src not in offm:
+            m = -1
+            for d in range(WORLD):
+                k = topo.mask(src, d) if d != src else 0
+                if k:
+                    m &= k
+            offm[src] = m
+        return offm[src]
+
+    def transfer(src, kind, c0, c1, dsts, sem, idx=0, parts=1):
+        m = -1
+        for d in dsts:
+            assert d != src and topo.may_write(src, d), (src, d)
+            m &= topo.mask(src, d)
+        if m & ~off_mask(src):
+            m &= ~off_mask(src)
+        b = _bits(m)
+        k = len(b) // parts
+        sel = b[idx * k:(idx + 1) * k]
+        for d in dsts:
+            total[(d, sem)] = total.get((d, sem), 0) + k
+        return (kind, c0, c1, list(dsts), sum(1 << i for i in sel), k, sem)
+
+    def op(core, prio, waits, planes, codes):
+        ops.setdefault(core, []).append((prio, waits, planes, codes))
+
+    relay, heavy = {}, {}
+    for r in range(n):
+        s, d = cores[r], cores[(r // GC) * GC + (1 - r % GC)]
+        near = lambda c: place(c) == place(s) and topo.may_write(c, d)
+        k0 = take(lambda c: near(c) and topo.die(c) == topo.die(s))
+        k1 = take(lambda c: near(c) and topo.die(c) != topo.die(s))
+        heavy[r] = k0 is None
+        if heavy[r]:
+            far = lambda c: (topo.chip(c) == topo.chip(s) and topo.may_write(s, c) and topo.may_write(c, d)
+                             and place(c) != place(s) and topo.die(c) != topo.die(s))
+            k0 = take(far)
+            k1 = take(lambda c: far(c) and topo.host(c) != topo.host(k0))
+        relay[r] = (k0, k1)
+        o = W * TA * (r % GC)
+        e1, e2 = o + W * A1, o + W * TA
+        h1, h2 = (o + e1) // 2, (e1 + e2) // 2
+        op(s, 0, [("za1", 1)],
+           [transfer(s, "a", o, e1, [k1], "a1")],
+           [transfer(s, "a", o, h1, [k1], "a1", 0, 2), transfer(s, "a", h1, e1, [k0], "a1", 1, 2)])
+        op(s, 2, [("za2", 1)],
+           [transfer(s, "a", e1, e2, [k0], "a2")],
+           [transfer(s, "a", e1, h2, [k1], "a2", 0, 2), transfer(s, "a", h2, e2, [k0], "a2", 1, 2)])
+        op(k1, 0, [("a1", None)], [transfer(k1, "a", o, e1, [d], "a1")], [transfer(k1, "a", o, h1, [d], "a1")])
+        op(k0, 0, [("a1", None)], [], [transfer(k0, "a", h1, e1, [d], "a1")])
+        op(k1, 2, [("a2", None)], [], [transfer(k1, "a", e1, h2, [d], "a2")])
+        op(k0, 2, [("a2", None)], [transfer(k0, "a", e1, e2, [d], "a2")], [transfer(k0, "a", h2, e2, [d], "a2")])
+
+    slot, when = {}, {}
+    for j in range(GC):
+        for k, r in enumerate(sorted((r for r in range(n) if r % GC == j), key=lambda r: cores[r])):
+            slot[r] = k
+    span = lambda r: (W * TB * slot[r], W * TB * (slot[r] + 1))
+    passes = []
+    for r in range(n):
+        s = cores[r]
+        peers = [p for p in range(n) if p % GC == r % GC and p != r]
+        direct = [p for p in peers if topo.may_write(s, cores[p])]
+        via = {}
+        for p in peers:
+            if p in direct:
+                continue
+            d = cores[p]
+            cand = [cores[f] for f in direct if not heavy[f] and topo.may_write(cores[f], d)]
+            isrank = bool(cand)
+            if not cand:
+                cand = [relay[f][1] for f in [r] + peers
+                        if not heavy[f] and topo.may_write(s, relay[f][1]) and topo.may_write(relay[f][1], d)]
+            cand.sort(key=lambda c: (place(c) != place(s) if not isrank else False, rack(c) != rack(d)))
+            via.setdefault((cand[0], isrank), []).append(d)
+        lead = [f for (f, _) in via]
+        for (f, isrank), ds in via.items():
+            passes.append((f, tuple(ds), r, isrank, place(f) == place(s)))
+            for d in ds:
+                when[(d, r)] = 4 if (isrank or place(f) == place(s)) else 7
+        rest = [cores[p] for p in direct if cores[p] not in lead]
+        for p in direct:
+            when[(cores[p], r)] = 1 if place(cores[p]) == place(s) else 2
+        late = [d for d in rest if heavy[r] and place(d) != place(s)]
+        for d in late:
+            when[(d, r)] = 4
+        first = lead + [d for d in rest if d not in late]
+        c0, c1 = span(r)
+        sem = "b%d" % (r // GC)
+        for prio, group in ((1, first), (3, late)):
+            sets = [x for x in ([d for d in group if place(d) != place(s)], [d for d in group if place(d) == place(s)]) if x]
+            if sets:
+                op(s, prio, [("zb", 1)], [transfer(s, "b", c0, c1, x, sem) for x in sets],
+                   [transfer(s, "b", c0, c1, x, sem) for x in sets])
+    done = set()
+    for i, (f, ds, r, isrank, home) in enumerate(passes):
+        if i in done:
+            continue
+        run = [r]
+        if isrank:
+            more = True
+            while more:
+                more = False
+                for k, (f2, ds2, r2, _, _) in enumerate(passes):
+                    if k != i and k not in done and f2 == f and ds2 == ds and r2 not in run and (
+                            slot[r2] == min(slot[x] for x in run) - 1 or slot[r2] == max(slot[x] for x in run) + 1):
+                        run.append(r2)
+                        done.add(k)
+                        more = True
+        c0, c1 = min(span(x)[0] for x in run), max(span(x)[1] for x in run)
+        sem = "b%d" % (run[0] // GC)
+        for x in run:
+            for d in ds:
+                when[(d, x)] = when[(d, x)] + (0.5 if len(run) > 1 else 0)
+        op(f, 4 if isrank else (1 if home else 3), [("b%d" % (x // GC), None) for x in run],
+           [transfer(f, "b", c0, c1, list(ds), sem)], [transfer(f, "b", c0, c1, list(ds), sem)])
+        for x in run[1:]:
+            for d in ds:
+                when[(d, x, "sem")] = sem
+
+    mm = {}
+    for r in range(n):
+        c, i, j = cores[r], r // GC, r % GC
+        items = []
+        for s in range(NS):
+            own_a = s // TA == j
+            first_a = s % TA < A1
+            asem = ("za1" if first_a else "za2") if own_a else ("a1" if first_a else "a2")
+            ka = 0 if own_a else (3 if first_a else 6)
+            src = (s // TB) * GC + j
+            if src == r:
+                bsem, kb = "zb", 0
+            else:
+                bsem, kb = when.get((c, src, "sem"), "b%d" % (s // TB)), when[(c, src)]
+            items.append((max(ka, kb), s, asem, bsem, W * s, W * TB * slot[src] + W * (s % TB)))
+        mm[r] = sorted(items)
+    for c in ops:
+        ops[c].sort(key=lambda x: x[0])
+    return {"ops": ops, "total": total, "mm": mm, "slot": slot}
+
+
+def rank_program(g, core, T, topo):
+    if "p" not in _CACHE:
+        _CACHE["p"] = make_plan(list(T.cores), topo)
+    plan = _CACHE["p"]
+    S, total = T.sem, plan["total"]
+    rank = T.rank_of(core)
+    need = lambda sem: total[(core, sem)] if (core, sem) in total else 1
+
+    if rank is not None:
+        j = rank % GC
+        o, ob = W * TA * j, W * TB * plan["slot"][rank]
+        e1, e2 = o + W * A1, o + W * TA
+        g.sync.dma_start(T.abf[:, 0:4 * W * A1], T.a[:, 0:4 * W * A1]).then_inc(S.la1, 16)
+        g.scalar.dma_start(T.bbf[:], T.b[:]).then_inc(S.lb, 16)
+        g.sync.dma_start(T.abf[:, 4 * W * A1:], T.a[:, 4 * W * A1:]).then_inc(S.la2, 16)
+        v = g.vector
+        v.wait_ge(S.la1, 16)
+        v.quantize_mx(T.qa[:, o:e1], T.sa[:, o:e1], T.abf[:, 0:4 * W * A1]).then_inc(S.za1, 1)
+        v.wait_ge(S.lb, 16)
+        v.quantize_mx(T.qb[:, ob:ob + W * TB], T.sb[:, ob:ob + W * TB], T.bbf[:]).then_inc(S.zb, 1)
+        v.wait_ge(S.la2, 16)
+        v.quantize_mx(T.qa[:, e1:e2], T.sa[:, e1:e2], T.abf[:, 4 * W * A1:]).then_inc(S.za2, 1)
+
+    left = 0
+    for _, waits, planes, codes in plan["ops"].get(core, []):
+        for sem, val in waits:
+            g.wait_ge(S[sem], val if val is not None else need(sem))
+        for is_codes, trs in ((False, planes), (True, codes)):
+            if not trs:
+                continue
+            call = []
+            for kind, c0, c1, dsts, mask, k, sem in trs:
+                ap = T["q" + kind][:, c0:c1].bitcast(dt.uint8) if is_codes else T["s" + kind][:, c0:c1]
+                ids = []
+                for d in dsts:
+                    rid, pid = topo.addr(d, core)
+                    ids.append(DstId(rid=rid, pnc=pid))
+                call.append(RemoteDMATransfer(dst_ids=ids, dma_engine_mask=mask, remote_sem=S[sem],
+                                              srcs=[ap], dsts=[ap for _ in dsts]))
+                left += k
+            g.remote_dma_fused(call, local_sem=S.ls)
+
+    if rank is not None:
+        t = g.tensor
+        seen = set()
+        items = plan["mm"][rank]
+        for n, (_, s, asem, bsem, ca, cb) in enumerate(items):
+            for sem in (asem, bsem):
+                if sem not in seen:
+                    seen.add(sem)
+                    t.wait_ge(S[sem], need(sem))
+            ins = t.matmul_mx(T.ps[:, 0:W], T.qa[:, ca:ca + W], T.sa[:, ca:ca + W], T.qb[:, cb:cb + W], T.sb[:, cb:cb + W],
+                              n == 0, n == len(items) - 1)
+        ins.then_inc(S.mm, 1)
+        g.vector.wait_ge(S.mm, 1)
+        g.vector.tensor_copy(T.yo[:], T.ps[:, 0:W]).then_inc(S.cp, 1)
+        g.sync.wait_ge(S.cp, 1)
+        g.sync.dma_start(T.y[:], T.yo[:]).then_inc(S.st, 16)
+        g.sync.wait_ge(S.st, 16)
+    if left:
+        g.wait_ge(S.ls, left)

@@ -4,7 +4,8 @@ from concourse.mybir import dt
 WORLD = 512
 GR, GC, NS = 5, 2, 10
 TA, TB, W = NS // GC, NS // GR, 128
-A1 = 2
+STEPS = ((0, TB), (TB, TA))
+NT = len(STEPS)
 
 SCRATCH = {
     "abf": ("sbuf", [128, TA * 4 * W], "bfloat16"),
@@ -16,7 +17,9 @@ SCRATCH = {
     "ps": ("psum", [128, 512], "float32"),
     "yo": ("sbuf", [128, W], "float32"),
 }
-SEMAPHORES = ["la1", "lb", "la2", "za1", "zb", "za2", "a1", "a2", "b0", "b1", "b2", "b3", "b4", "ls", "mm", "cp", "st"]
+SEMAPHORES = (["lb", "zb", "ls", "mm", "cp", "st"]
+              + [p + str(t) for p in ("la", "za", "pa", "a") for t in range(NT)]
+              + [p + str(i) for p in ("pb", "b") for i in range(GR)])
 
 _CACHE = {}
 
@@ -30,156 +33,176 @@ def make_plan(cores, topo):
     used = set(cores)
     place = lambda c: (topo.host(c), topo.chip(c))
     rack = lambda c: topo.rack(topo.host(c))
+    cable = lambda c: c // 2
+    ops, total, load = {}, {}, {}
 
-    def take(pred):
-        for c in range(WORLD):
-            if c not in used and pred(c):
-                used.add(c)
-                return c
-        return None
+    def link(c, d):
+        if place(c) == place(d):
+            return None
+        if rack(c) != rack(d):
+            return ("cable", cable(c))
+        return ("mate" if topo.mates(c, d) else "switch", place(d), topo.die(c))
 
-    ops, total, offm = {}, {}, {}
+    def charge(c, dsts, cols):
+        for d in dsts:
+            if link(c, d):
+                load[link(c, d)] = load.get(link(c, d), 0) + cols
 
-    def off_mask(src):
-        if src not in offm:
+    def take(pred, dsts=()):
+        cand = [c for c in range(WORLD) if c not in used and pred(c)]
+        c = min(cand, key=lambda c: (sum(load.get(link(c, d), 0) for d in dsts), c))
+        used.add(c)
+        return c
+
+    def call(src, items):
+        allow = []
+        for _, _, _, dsts, _ in items:
             m = -1
-            for d in range(WORLD):
-                k = topo.mask(src, d) if d != src else 0
-                if k:
-                    m &= k
-            offm[src] = m
-        return offm[src]
+            for d in dsts:
+                assert d != src and topo.may_write(src, d), (src, d)
+                m &= topo.mask(src, d)
+            allow.append(m)
+        common = -1
+        for m in allow:
+            common &= m
+        if any(m == common for m in allow):
+            allow = [m if m == common else m & ~common for m in allow]
+        out = []
+        for i, (kind, c0, c1, dsts, sem) in enumerate(items):
+            same = [k for k, m in enumerate(allow) if m == allow[i]]
+            b = _bits(allow[i])
+            k = len(b) // len(same)
+            sel = b[same.index(i) * k:(same.index(i) + 1) * k]
+            for d in dsts:
+                total[(d, sem)] = total.get((d, sem), 0) + k
+            out.append((kind, c0, c1, list(dsts), sum(1 << x for x in sel), k, sem))
+        return out
 
-    def transfer(src, kind, c0, c1, dsts, sem, idx=0, parts=1):
-        m = -1
-        for d in dsts:
-            assert d != src and topo.may_write(src, d), (src, d)
-            m &= topo.mask(src, d)
-        if m & ~off_mask(src):
-            m &= ~off_mask(src)
-        b = _bits(m)
-        k = len(b) // parts
-        sel = b[idx * k:(idx + 1) * k]
-        for d in dsts:
-            total[(d, sem)] = total.get((d, sem), 0) + k
-        return (kind, c0, c1, list(dsts), sum(1 << i for i in sel), k, sem)
+    def op(core, prio, pw, planes, cw, codes):
+        ops.setdefault(core, []).append((prio, pw, planes, cw, codes))
 
-    def op(core, prio, waits, planes, codes):
-        ops.setdefault(core, []).append((prio, waits, planes, codes))
+    def passes(k, prio, kind, c0, c1, groups, ps, cs):
+        op(k, prio, [(ps, None)], call(k, [(kind, c0, c1, x, ps) for x in groups]),
+           [(cs, None)], call(k, [(kind, c0, c1, x, cs) for x in groups]))
 
-    relay, heavy = {}, {}
+    partner = lambda r: (r // GC) * GC + (1 - r % GC)
+    heavy = {r: not any(place(c) == place(cores[r]) and c != cores[r] and topo.may_write(c, cores[partner(r)])
+                        for c in range(WORLD)) for r in range(n)}
+    relay = {}
     for r in range(n):
-        s, d = cores[r], cores[(r // GC) * GC + (1 - r % GC)]
-        near = lambda c: place(c) == place(s) and topo.may_write(c, d)
-        k0 = take(lambda c: near(c) and topo.die(c) == topo.die(s))
-        k1 = take(lambda c: near(c) and topo.die(c) != topo.die(s))
-        heavy[r] = k0 is None
+        if not heavy[r]:
+            s, d = cores[r], cores[partner(r)]
+            near = lambda c: place(c) == place(s) and topo.may_write(c, d)
+            relay[r] = [take(lambda c: near(c) and topo.die(c) == topo.die(s)),
+                        take(lambda c: near(c) and topo.die(c) != topo.die(s))]
+    busy = set(cable(c) for c in cores)
+    for r in range(n):
         if heavy[r]:
-            far = lambda c: (topo.chip(c) == topo.chip(s) and topo.may_write(s, c) and topo.may_write(c, d)
-                             and place(c) != place(s) and topo.die(c) != topo.die(s))
-            k0 = take(far)
-            k1 = take(lambda c: far(c) and topo.host(c) != topo.host(k0))
-        relay[r] = (k0, k1)
+            s, d = cores[r], cores[partner(r)]
+            relay[r] = []
+            for _ in range(3):
+                k = take(lambda c: (topo.same_plane(s, c) and topo.chip(c) == topo.chip(d) and rack(c) != rack(d)
+                                    and topo.may_write(s, c) and topo.may_write(c, d) and cable(c) not in busy))
+                busy.add(cable(k))
+                relay[r].append(k)
+    first = {}
+    for r in range(n):
+        s, d, R = cores[r], cores[partner(r)], relay[r]
         o = W * TA * (r % GC)
-        e1, e2 = o + W * A1, o + W * TA
-        h1, h2 = (o + e1) // 2, (e1 + e2) // 2
-        op(s, 0, [("za1", 1)],
-           [transfer(s, "a", o, e1, [k1], "a1")],
-           [transfer(s, "a", o, h1, [k1], "a1", 0, 2), transfer(s, "a", h1, e1, [k0], "a1", 1, 2)])
-        op(s, 2, [("za2", 1)],
-           [transfer(s, "a", e1, e2, [k0], "a2")],
-           [transfer(s, "a", e1, h2, [k1], "a2", 0, 2), transfer(s, "a", h2, e2, [k0], "a2", 1, 2)])
-        op(k1, 0, [("a1", None)], [transfer(k1, "a", o, e1, [d], "a1")], [transfer(k1, "a", o, h1, [d], "a1")])
-        op(k0, 0, [("a1", None)], [], [transfer(k0, "a", h1, e1, [d], "a1")])
-        op(k1, 2, [("a2", None)], [], [transfer(k1, "a", e1, h2, [d], "a2")])
-        op(k0, 2, [("a2", None)], [transfer(k0, "a", e1, e2, [d], "a2")], [transfer(k0, "a", h2, e2, [d], "a2")])
+        c0, c1 = o + W * STEPS[0][0], o + W * STEPS[0][1]
+        part = {R[0]: (c0, c0 + W), R[-1]: (c0 + W, c1)}
+        first[r] = ([("a", c0, c1, [R[1]], "pa0")], [("a", x0, x1, [k], "a0") for k, (x0, x1) in part.items()])
+        for k in R:
+            op(k, 0, [("pa0", None)], call(k, [("a", c0, c1, [d], "pa0")]) if k == R[1] else [],
+               [("a0", None)], call(k, [("a", part[k][0], part[k][1], [d], "a0")]) if k in part else [])
+            x = (4 * W if k in part else 0) + (c1 - c0 if k == R[1] else 0)
+            charge(s, [k], x)
+            charge(k, [d], x)
+        c0, c1 = o + W * STEPS[1][0], o + W * STEPS[1][1]
+        w = (c1 - c0) // len(R)
+        shares = [(k, c0 + q * w, c0 + (q + 1) * w) for q, k in enumerate(R)]
+        op(s, 1, [("za1", 1)], call(s, [("a", x0, x1, [k], "pa1") for k, x0, x1 in shares]),
+           [], call(s, [("a", x0, x1, [k], "a1") for k, x0, x1 in shares]))
+        for k, x0, x1 in shares:
+            passes(k, 1, "a", x0, x1, [[d]], "pa1", "a1")
+            charge(s, [k], 5 * (x1 - x0))
+            charge(k, [d], 5 * (x1 - x0))
 
-    slot, when = {}, {}
-    for j in range(GC):
-        for k, r in enumerate(sorted((r for r in range(n) if r % GC == j), key=lambda r: cores[r])):
-            slot[r] = k
-    span = lambda r: (W * TB * slot[r], W * TB * (slot[r] + 1))
-    passes = []
+    when, jobs, firsts = {}, [], {}
+    cols = 5 * W * TB
     for r in range(n):
         s = cores[r]
         peers = [p for p in range(n) if p % GC == r % GC and p != r]
-        direct = [p for p in peers if topo.may_write(s, cores[p])]
-        via = {}
-        for p in peers:
-            if p in direct:
-                continue
-            d = cores[p]
-            cand = [cores[f] for f in direct if not heavy[f] and topo.may_write(cores[f], d)]
-            isrank = bool(cand)
-            if not cand:
-                cand = [relay[f][1] for f in [r] + peers
-                        if not heavy[f] and topo.may_write(s, relay[f][1]) and topo.may_write(relay[f][1], d)]
-            cand.sort(key=lambda c: (place(c) != place(s) if not isrank else False, rack(c) != rack(d)))
-            via.setdefault((cand[0], isrank), []).append(d)
-        lead = [f for (f, _) in via]
-        for (f, isrank), ds in via.items():
-            passes.append((f, tuple(ds), r, isrank, place(f) == place(s)))
-            for d in ds:
-                when[(d, r)] = 4 if (isrank or place(f) == place(s)) else 7
-        rest = [cores[p] for p in direct if cores[p] not in lead]
-        for p in direct:
+        far = [p for p in peers if rack(cores[p]) != rack(s)]
+        near = [p for p in peers if p not in far]
+        trees = []
+        land = [q for q in far if topo.chip(cores[q]) == topo.chip(s) and topo.may_write(s, cores[q])]
+        if land:
+            trees.append((lambda c, q=cores[land[0]]: place(c) == place(q), far))
+        else:
+            for q in far:
+                p = [p for p in near if topo.chip(cores[p]) == topo.chip(cores[q]) and topo.may_write(cores[p], cores[q])][0]
+                trees.append((lambda c, p=cores[p]: place(c) == place(p), [p, q]))
+                near.remove(p)
+        for p in [p for p in near if not topo.may_write(s, cores[p])]:
+            trees.append((lambda c, p=cores[p]: topo.mates(c, p), [p]))
+            near.remove(p)
+        out = [p for p in near if place(cores[p]) != place(s)]
+        if out and len(trees) + len(out) + (1 if heavy[r] else 0) > 2:
+            trees.append((lambda c, s=s: place(c) == place(s), out))
+            near = [p for p in near if p not in out]
+        firsts[r] = [cores[p] for p in near]
+        for p in near:
             when[(cores[p], r)] = 1 if place(cores[p]) == place(s) else 2
-        late = [d for d in rest if heavy[r] and place(d) != place(s)]
-        for d in late:
-            when[(d, r)] = 4
-        first = lead + [d for d in rest if d not in late]
-        c0, c1 = span(r)
-        sem = "b%d" % (r // GC)
-        for prio, group in ((1, first), (3, late)):
-            sets = [x for x in ([d for d in group if place(d) != place(s)], [d for d in group if place(d) == place(s)]) if x]
-            if sets:
-                op(s, prio, [("zb", 1)], [transfer(s, "b", c0, c1, x, sem) for x in sets],
-                   [transfer(s, "b", c0, c1, x, sem) for x in sets])
-    done = set()
-    for i, (f, ds, r, isrank, home) in enumerate(passes):
-        if i in done:
-            continue
-        run = [r]
-        if isrank:
-            more = True
-            while more:
-                more = False
-                for k, (f2, ds2, r2, _, _) in enumerate(passes):
-                    if k != i and k not in done and f2 == f and ds2 == ds and r2 not in run and (
-                            slot[r2] == min(slot[x] for x in run) - 1 or slot[r2] == max(slot[x] for x in run) + 1):
-                        run.append(r2)
-                        done.add(k)
-                        more = True
-        c0, c1 = min(span(x)[0] for x in run), max(span(x)[1] for x in run)
-        sem = "b%d" % (run[0] // GC)
-        for x in run:
+        charge(s, firsts[r], cols)
+        for where, serves in trees:
+            ds = [cores[p] for p in serves]
+            pred = lambda c, where=where, ds=ds, s=s: (where(c) and topo.may_write(s, c)
+                                                       and all(topo.may_write(c, d) for d in ds))
+            cand = [c for c in range(WORLD) if c not in used and pred(c)]
+            charge(s, cand[:1], cols)
+            jobs.append((len(cand), r, pred, ds))
+    spread = {}
+    for _, r, pred, ds in sorted(jobs, key=lambda x: x[:2]):
+        h = take(pred, ds)
+        charge(h, ds, cols)
+        spread.setdefault(r, []).append((h, ds))
+    for r in range(n):
+        s, i = cores[r], r // GC
+        c0, c1 = W * TB * i, W * TB * (i + 1)
+        ps, cs = "pb%d" % i, "b%d" % i
+        groups = lambda src, dsts: [x for x in ([d for d in dsts if place(d) != place(src)],
+                                                [d for d in dsts if place(d) == place(src)]) if x]
+        hs = sorted(spread.get(r, []), key=lambda x: (place(x[0]) == place(s), rack(x[0]) == rack(s)))
+        dsts = [h for h, _ in hs] + firsts[r]
+        op(s, 0, [("zb", 1), ("za0", 1)], call(s, [("b", c0, c1, x, ps) for x in groups(s, dsts)] + first[r][0]),
+           [], call(s, [("b", y, y + W, x, cs) for x in groups(s, dsts) for y in range(c0, c1, W)] + first[r][1]))
+        for h, ds in hs:
+            ds = sorted(ds, key=lambda d: rack(d) == rack(h))
+            passes(h, 0, "b", c0, c1, groups(h, ds), ps, cs)
             for d in ds:
-                when[(d, x)] = when[(d, x)] + (0.5 if len(run) > 1 else 0)
-        op(f, 4 if isrank else (1 if home else 3), [("b%d" % (x // GC), None) for x in run],
-           [transfer(f, "b", c0, c1, list(ds), sem)], [transfer(f, "b", c0, c1, list(ds), sem)])
-        for x in run[1:]:
-            for d in ds:
-                when[(d, x, "sem")] = sem
+                when[(d, r)] = 3 if place(h) == place(s) else (4 if place(d) == place(h) else 4.5)
 
     mm = {}
     for r in range(n):
-        c, i, j = cores[r], r // GC, r % GC
+        c, j = cores[r], r % GC
         items = []
         for s in range(NS):
-            own_a = s // TA == j
-            first_a = s % TA < A1
-            asem = ("za1" if first_a else "za2") if own_a else ("a1" if first_a else "a2")
-            ka = 0 if own_a else (3 if first_a else 6)
+            t = [k for k, (t0, t1) in enumerate(STEPS) if t0 <= s % TA < t1][0]
+            if s // TA == j:
+                sems, ka = ["za%d" % t], 0.3 * t
+            else:
+                sems, ka = ["pa%d" % t, "a%d" % t], 4.2 + 2 * t
             src = (s // TB) * GC + j
             if src == r:
-                bsem, kb = "zb", 0
+                sems, kb = sems + ["zb"], 0
             else:
-                bsem, kb = when.get((c, src, "sem"), "b%d" % (s // TB)), when[(c, src)]
-            items.append((max(ka, kb), s, asem, bsem, W * s, W * TB * slot[src] + W * (s % TB)))
+                sems, kb = sems + ["pb%d" % (s // TB), "b%d" % (s // TB)], when[(c, src)]
+            items.append((max(ka, kb), s, sems))
         mm[r] = sorted(items)
     for c in ops:
         ops[c].sort(key=lambda x: x[0])
-    return {"ops": ops, "total": total, "mm": mm, "slot": slot}
+    return {"ops": ops, "total": total, "mm": mm, "load": load}
 
 
 def rank_program(g, core, T, topo):
@@ -191,49 +214,49 @@ def rank_program(g, core, T, topo):
     need = lambda sem: total[(core, sem)] if (core, sem) in total else 1
 
     if rank is not None:
-        j = rank % GC
-        o, ob = W * TA * j, W * TB * plan["slot"][rank]
-        e1, e2 = o + W * A1, o + W * TA
-        g.sync.dma_start(T.abf[:, 0:4 * W * A1], T.a[:, 0:4 * W * A1]).then_inc(S.la1, 16)
-        g.scalar.dma_start(T.bbf[:], T.b[:]).then_inc(S.lb, 16)
-        g.sync.dma_start(T.abf[:, 4 * W * A1:], T.a[:, 4 * W * A1:]).then_inc(S.la2, 16)
+        o, ob = W * TA * (rank % GC), W * TB * (rank // GC)
+        g.sync.dma_start(T.bbf[:], T.b[:]).then_inc(S.lb, 16)
+        for t, (t0, t1) in enumerate(STEPS):
+            q = g.scalar if t % 2 == 0 else g.sync
+            q.dma_start(T.abf[:, 4 * W * t0:4 * W * t1], T.a[:, 4 * W * t0:4 * W * t1]).then_inc(S["la%d" % t], 16)
         v = g.vector
-        v.wait_ge(S.la1, 16)
-        v.quantize_mx(T.qa[:, o:e1], T.sa[:, o:e1], T.abf[:, 0:4 * W * A1]).then_inc(S.za1, 1)
         v.wait_ge(S.lb, 16)
         v.quantize_mx(T.qb[:, ob:ob + W * TB], T.sb[:, ob:ob + W * TB], T.bbf[:]).then_inc(S.zb, 1)
-        v.wait_ge(S.la2, 16)
-        v.quantize_mx(T.qa[:, e1:e2], T.sa[:, e1:e2], T.abf[:, 4 * W * A1:]).then_inc(S.za2, 1)
+        for t, (t0, t1) in enumerate(STEPS):
+            v.wait_ge(S["la%d" % t], 16)
+            v.quantize_mx(T.qa[:, o + W * t0:o + W * t1], T.sa[:, o + W * t0:o + W * t1],
+                          T.abf[:, 4 * W * t0:4 * W * t1]).then_inc(S["za%d" % t], 1)
 
     left = 0
-    for _, waits, planes, codes in plan["ops"].get(core, []):
-        for sem, val in waits:
-            g.wait_ge(S[sem], val if val is not None else need(sem))
-        for is_codes, trs in ((False, planes), (True, codes)):
+    for _, pw, planes, cw, codes in plan["ops"].get(core, []):
+        for is_codes, waits, trs in ((False, pw, planes), (True, cw, codes)):
             if not trs:
                 continue
-            call = []
+            for sem, val in waits:
+                g.wait_ge(S[sem], val if val is not None else need(sem))
+            fused = []
             for kind, c0, c1, dsts, mask, k, sem in trs:
                 ap = T["q" + kind][:, c0:c1].bitcast(dt.uint8) if is_codes else T["s" + kind][:, c0:c1]
                 ids = []
                 for d in dsts:
                     rid, pid = topo.addr(d, core)
                     ids.append(DstId(rid=rid, pnc=pid))
-                call.append(RemoteDMATransfer(dst_ids=ids, dma_engine_mask=mask, remote_sem=S[sem],
-                                              srcs=[ap], dsts=[ap for _ in dsts]))
+                fused.append(RemoteDMATransfer(dst_ids=ids, dma_engine_mask=mask, remote_sem=S[sem],
+                                               srcs=[ap], dsts=[ap for _ in dsts]))
                 left += k
-            g.remote_dma_fused(call, local_sem=S.ls)
+            g.remote_dma_fused(fused, local_sem=S.ls)
 
     if rank is not None:
         t = g.tensor
         seen = set()
         items = plan["mm"][rank]
-        for n, (_, s, asem, bsem, ca, cb) in enumerate(items):
-            for sem in (asem, bsem):
+        for n, (_, s, sems) in enumerate(items):
+            for sem in sems:
                 if sem not in seen:
                     seen.add(sem)
                     t.wait_ge(S[sem], need(sem))
-            ins = t.matmul_mx(T.ps[:, 0:W], T.qa[:, ca:ca + W], T.sa[:, ca:ca + W], T.qb[:, cb:cb + W], T.sb[:, cb:cb + W],
+            c = W * s
+            ins = t.matmul_mx(T.ps[:, 0:W], T.qa[:, c:c + W], T.sa[:, c:c + W], T.qb[:, c:c + W], T.sb[:, c:c + W],
                               n == 0, n == len(items) - 1)
         ins.then_inc(S.mm, 1)
         g.vector.wait_ge(S.mm, 1)

from concourse.bass import DstId, RemoteDMATransfer
from concourse.mybir import dt

WORLD = 512
GR, GC, NS = 5, 2, 10
TA, TB, W = NS // GC, NS // GR, 128
STEPS = ((0, TB), (TB, TA))
NT = len(STEPS)

SCRATCH = {
    "abf": ("sbuf", [128, TA * 4 * W], "bfloat16"),
    "bbf": ("sbuf", [128, TB * 4 * W], "bfloat16"),
    "qa": ("sbuf", [128, NS * W], "float8_e4m3fn_x4"),
    "sa": ("sbuf", [128, NS * W], "uint8"),
    "qb": ("sbuf", [128, NS * W], "float8_e4m3fn_x4"),
    "sb": ("sbuf", [128, NS * W], "uint8"),
    "ps": ("psum", [128, 512], "float32"),
    "yo": ("sbuf", [128, W], "float32"),
}
SEMAPHORES = (["lb", "zb", "ls", "mm", "cp", "st"]
              + [p + str(t) for p in ("la", "za", "pa", "a") for t in range(NT)]
              + [p + str(i) for p in ("pb", "b") for i in range(GR)])

_CACHE = {}


def _bits(m):
    return [i for i in range(m.bit_length()) if (m >> i) & 1]


def make_plan(cores, topo):
    n = len(cores)
    used = set(cores)
    place = lambda c: (topo.host(c), topo.chip(c))
    rack = lambda c: topo.rack(topo.host(c))
    cable = lambda c: c // 2
    ops, total, load = {}, {}, {}

    def link(c, d):
        if place(c) == place(d):
            return None
        if rack(c) != rack(d):
            return ("cable", cable(c))
        return ("mate" if topo.mates(c, d) else "switch", place(d), topo.die(c))

    def charge(c, dsts, cols):
        for d in dsts:
            if link(c, d):
                load[link(c, d)] = load.get(link(c, d), 0) + cols

    def take(pred, dsts=()):
        cand = [c for c in range(WORLD) if c not in used and pred(c)]
        c = min(cand, key=lambda c: (sum(load.get(link(c, d), 0) for d in dsts), c))
        used.add(c)
        return c

    def call(src, items):
        allow = []
        for _, _, _, dsts, _ in items:
            m = -1
            for d in dsts:
                assert d != src and topo.may_write(src, d), (src, d)
                m &= topo.mask(src, d)
            allow.append(m)
        common = -1
        for m in allow:
            common &= m
        if any(m == common for m in allow):
            allow = [m if m == common else m & ~common for m in allow]
        out = []
        for i, (kind, c0, c1, dsts, sem) in enumerate(items):
            same = [k for k, m in enumerate(allow) if m == allow[i]]
            b = _bits(allow[i])
            k = len(b) // len(same)
            sel = b[same.index(i) * k:(same.index(i) + 1) * k]
            for d in dsts:
                total[(d, sem)] = total.get((d, sem), 0) + k
            out.append((kind, c0, c1, list(dsts), sum(1 << x for x in sel), k, sem))
        return out

    def op(core, prio, pw, planes, cw, codes):
        ops.setdefault(core, []).append((prio, pw, planes, cw, codes))

    def passes(k, prio, kind, c0, c1, groups, ps, cs):
        op(k, prio, [(ps, None)], call(k, [(kind, c0, c1, x, ps) for x in groups]),
           [(cs, None)], call(k, [(kind, c0, c1, x, cs) for x in groups]))

    partner = lambda r: (r // GC) * GC + (1 - r % GC)
    heavy = {r: not any(place(c) == place(cores[r]) and c != cores[r] and topo.may_write(c, cores[partner(r)])
                        for c in range(WORLD)) for r in range(n)}
    relay = {}
    for r in range(n):
        if not heavy[r]:
            s, d = cores[r], cores[partner(r)]
            near = lambda c: place(c) == place(s) and topo.may_write(c, d)
            relay[r] = [take(lambda c: near(c) and topo.die(c) == topo.die(s)),
                        take(lambda c: near(c) and topo.die(c) != topo.die(s))]
    busy = set(cable(c) for c in cores)
    for r in range(n):
        if heavy[r]:
            s, d = cores[r], cores[partner(r)]
            relay[r] = []
            for _ in range(3):
                k = take(lambda c: (topo.same_plane(s, c) and topo.chip(c) == topo.chip(d) and rack(c) != rack(d)
                                    and topo.may_write(s, c) and topo.may_write(c, d) and cable(c) not in busy))
                busy.add(cable(k))
                relay[r].append(k)
    first = {}
    for r in range(n):
        s, d, R = cores[r], cores[partner(r)], relay[r]
        o = W * TA * (r % GC)
        c0, c1 = o + W * STEPS[0][0], o + W * STEPS[0][1]
        part = {R[0]: (c0, c0 + W), R[-1]: (c0 + W, c1)}
        first[r] = ([("a", c0, c1, [R[1]], "pa0")], [("a", x0, x1, [k], "a0") for k, (x0, x1) in part.items()])
        for k in R:
            op(k, 0, [("pa0", None)], call(k, [("a", c0, c1, [d], "pa0")]) if k == R[1] else [],
               [("a0", None)], call(k, [("a", part[k][0], part[k][1], [d], "a0")]) if k in part else [])
            x = (4 * W if k in part else 0) + (c1 - c0 if k == R[1] else 0)
            charge(s, [k], x)
            charge(k, [d], x)
        c0, c1 = o + W * STEPS[1][0], o + W * STEPS[1][1]
        w = (c1 - c0) // len(R)
        shares = [(k, c0 + q * w, c0 + (q + 1) * w) for q, k in enumerate(R)]
        op(s, 1, [("za1", 1)], call(s, [("a", x0, x1, [k], "pa1") for k, x0, x1 in shares]),
           [], call(s, [("a", x0, x1, [k], "a1") for k, x0, x1 in shares]))
        for k, x0, x1 in shares:
            passes(k, 1, "a", x0, x1, [[d]], "pa1", "a1")
            charge(s, [k], 5 * (x1 - x0))
            charge(k, [d], 5 * (x1 - x0))

    when, jobs, firsts = {}, [], {}
    cols = 5 * W * TB
    for r in range(n):
        s = cores[r]
        peers = [p for p in range(n) if p % GC == r % GC and p != r]
        far = [p for p in peers if rack(cores[p]) != rack(s)]
        near = [p for p in peers if p not in far]
        trees = []
        land = [q for q in far if topo.chip(cores[q]) == topo.chip(s) and topo.may_write(s, cores[q])]
        if land:
            trees.append((lambda c, q=cores[land[0]]: place(c) == place(q), far))
        else:
            for q in far:
                p = [p for p in near if topo.chip(cores[p]) == topo.chip(cores[q]) and topo.may_write(cores[p], cores[q])][0]
                trees.append((lambda c, p=cores[p]: place(c) == place(p), [p, q]))
                near.remove(p)
        for p in [p for p in near if not topo.may_write(s, cores[p])]:
            trees.append((lambda c, p=cores[p]: topo.mates(c, p), [p]))
            near.remove(p)
        out = [p for p in near if place(cores[p]) != place(s)]
        if out and len(trees) + len(out) + (1 if heavy[r] else 0) > 2:
            trees.append((lambda c, s=s: place(c) == place(s), out))
            near = [p for p in near if p not in out]
        firsts[r] = [cores[p] for p in near]
        for p in near:
            when[(cores[p], r)] = 1 if place(cores[p]) == place(s) else 2
        charge(s, firsts[r], cols)
        for where, serves in trees:
            ds = [cores[p] for p in serves]
            pred = lambda c, where=where, ds=ds, s=s: (where(c) and topo.may_write(s, c)
                                                       and all(topo.may_write(c, d) for d in ds))
            cand = [c for c in range(WORLD) if c not in used and pred(c)]
            charge(s, cand[:1], cols)
            jobs.append((len(cand), r, pred, ds))
    spread = {}
    for _, r, pred, ds in sorted(jobs, key=lambda x: x[:2]):
        h = take(pred, ds)
        charge(h, ds, cols)
        spread.setdefault(r, []).append((h, ds))
    for r in range(n):
        s, i = cores[r], r // GC
        c0, c1 = W * TB * i, W * TB * (i + 1)
        ps, cs = "pb%d" % i, "b%d" % i
        groups = lambda src, dsts: [x for x in ([d for d in dsts if place(d) != place(src)],
                                                [d for d in dsts if place(d) == place(src)]) if x]
        hs = sorted(spread.get(r, []), key=lambda x: (place(x[0]) == place(s), rack(x[0]) == rack(s)))
        dsts = [h for h, _ in hs] + firsts[r]
        op(s, 0, [("zb", 1), ("za0", 1)], call(s, [("b", c0, c1, x, ps) for x in groups(s, dsts)] + first[r][0]),
           [], call(s, [("b", y, y + W, x, cs) for x in groups(s, dsts) for y in range(c0, c1, W)] + first[r][1]))
        for h, ds in hs:
            ds = sorted(ds, key=lambda d: rack(d) == rack(h))
            passes(h, 0, "b", c0, c1, groups(h, ds), ps, cs)
            for d in ds:
                when[(d, r)] = 3 if place(h) == place(s) else (4 if place(d) == place(h) else 4.5)

    mm = {}
    for r in range(n):
        c, j = cores[r], r % GC
        items = []
        for s in range(NS):
            t = [k for k, (t0, t1) in enumerate(STEPS) if t0 <= s % TA < t1][0]
            if s // TA == j:
                sems, ka = ["za%d" % t], 0.3 * t
            else:
                sems, ka = ["pa%d" % t, "a%d" % t], 4.2 + 2 * t
            src = (s // TB) * GC + j
            if src == r:
                sems, kb = sems + ["zb"], 0
            else:
                sems, kb = sems + ["pb%d" % (s // TB), "b%d" % (s // TB)], when[(c, src)]
            items.append((max(ka, kb), s, sems))
        mm[r] = sorted(items)
    for c in ops:
        ops[c].sort(key=lambda x: x[0])
    return {"ops": ops, "total": total, "mm": mm, "load": load}


def rank_program(g, core, T, topo):
    if "p" not in _CACHE:
        _CACHE["p"] = make_plan(list(T.cores), topo)
    plan = _CACHE["p"]
    S, total = T.sem, plan["total"]
    rank = T.rank_of(core)
    need = lambda sem: total[(core, sem)] if (core, sem) in total else 1

    if rank is not None:
        o, ob = W * TA * (rank % GC), W * TB * (rank // GC)
        g.sync.dma_start(T.bbf[:], T.b[:]).then_inc(S.lb, 16)
        for t, (t0, t1) in enumerate(STEPS):
            q = g.scalar if t % 2 == 0 else g.sync
            q.dma_start(T.abf[:, 4 * W * t0:4 * W * t1], T.a[:, 4 * W * t0:4 * W * t1]).then_inc(S["la%d" % t], 16)
        v = g.vector
        v.wait_ge(S.lb, 16)
        v.quantize_mx(T.qb[:, ob:ob + W * TB], T.sb[:, ob:ob + W * TB], T.bbf[:]).then_inc(S.zb, 1)
        for t, (t0, t1) in enumerate(STEPS):
            v.wait_ge(S["la%d" % t], 16)
            v.quantize_mx(T.qa[:, o + W * t0:o + W * t1], T.sa[:, o + W * t0:o + W * t1],
                          T.abf[:, 4 * W * t0:4 * W * t1]).then_inc(S["za%d" % t], 1)

    left = 0
    for _, pw, planes, cw, codes in plan["ops"].get(core, []):
        for is_codes, waits, trs in ((False, pw, planes), (True, cw, codes)):
            if not trs:
                continue
            for sem, val in waits:
                g.wait_ge(S[sem], val if val is not None else need(sem))
            fused = []
            for kind, c0, c1, dsts, mask, k, sem in trs:
                ap = T["q" + kind][:, c0:c1].bitcast(dt.uint8) if is_codes else T["s" + kind][:, c0:c1]
                ids = []
                for d in dsts:
                    rid, pid = topo.addr(d, core)
                    ids.append(DstId(rid=rid, pnc=pid))
                fused.append(RemoteDMATransfer(dst_ids=ids, dma_engine_mask=mask, remote_sem=S[sem],
                                               srcs=[ap], dsts=[ap for _ in dsts]))
                left += k
            g.remote_dma_fused(fused, local_sem=S.ls)

    if rank is not None:
        t = g.tensor
        seen = set()
        items = plan["mm"][rank]
        for n, (_, s, sems) in enumerate(items):
            for sem in sems:
                if sem not in seen:
                    seen.add(sem)
                    t.wait_ge(S[sem], need(sem))
            c = W * s
            ins = t.matmul_mx(T.ps[:, 0:W], T.qa[:, c:c + W], T.sa[:, c:c + W], T.qb[:, c:c + W], T.sb[:, c:c + W],
                              n == 0, n == len(items) - 1)
        ins.then_inc(S.mm, 1)
        g.vector.wait_ge(S.mm, 1)
        g.vector.tensor_copy(T.yo[:], T.ps[:, 0:W]).then_inc(S.cp, 1)
        g.sync.wait_ge(S.cp, 1)
        g.sync.dma_start(T.y[:], T.yo[:]).then_inc(S.st, 16)
        g.sync.wait_ge(S.st, 16)
    if left:
        g.wait_ge(S.ls, left)
